import numpy as np
import ml_dtypes


def mxq(x, axis, fmt="e4m3"):
    dtype, down = {"e4m3": (ml_dtypes.float8_e4m3fn, 7), "e5m2": (ml_dtypes.float8_e5m2, 14)}[fmt]
    v = np.moveaxis(np.asarray(x, np.float32).astype(ml_dtypes.bfloat16).astype(np.float64), axis, -1)
    blocks = v.reshape(v.shape[:-1] + (-1, 32))
    amax = np.abs(blocks).max(-1, keepdims=True)
    byte = np.maximum(np.where(amax > 0, np.frexp(amax)[1] - 1 + 127, 0) - down, 1)
    scale = np.exp2(byte - 127.0)
    codes = (blocks / scale).astype(np.float32).astype(dtype).astype(np.float64)
    return np.moveaxis((codes * scale).reshape(v.shape), -1, axis)


WIDE = False


def mx_kscale(k):
    if not WIDE:
        return np.ones(k)
    levels = np.array([10, -10, 5, -5, 0])
    if k % 512:
        return np.exp2(np.random.permutation(np.resize(levels, k // 32))).repeat(32)
    a = np.empty((k // 512, 16))
    for p in range(k // 512):
        a[p, :8] = np.random.permutation(np.resize(levels, 8))
        for g in range(8):
            far = levels[np.abs(levels - a[p, g]) >= 10]
            a[p, g + 8] = far[np.random.randint(len(far))]
    return np.exp2(a.ravel()).repeat(32)


def f64(x):
    return np.asarray(x).astype(np.float64)


def striped8(idx):
    return np.asarray(idx).reshape(8, -1, 16).transpose(0, 2, 1).reshape(128, -1).astype(np.uint16)


def unstriped8(offs):
    return offs.reshape(8, 16, -1).transpose(0, 2, 1).reshape(8, -1).astype(np.int64)


def pick8(x, idx, run):
    r = np.arange(len(x))
    return x[r[:, None], idx[r % (8 * run) // run]]


E2M1 = np.array([0.0, 0.5, 1.0, 1.5, 2.0, 3.0, 4.0, 6.0, -0.0, -0.5, -1.0, -1.5, -2.0, -3.0, -4.0, -6.0])


def pack_weight(w, fmt):
    k, n = w.shape
    w = f64(np.asarray(w, np.float32).astype(ml_dtypes.bfloat16)).reshape(k // 32, 32, n)
    amax = np.abs(w).max(1)
    if fmt == "e4m3":
        byte = np.frexp(amax)[1] - 1 + 127 - 7
    else:
        mant, ex = np.frexp(amax / 6.0)
        byte = np.where(mant > 0.5, ex, ex - 1) + 127
    byte = np.clip(np.where(amax > 0, byte, 1), 1, 254)
    scaled = (w * np.exp2(127.0 - byte)[:, None, :]).reshape(k, n).astype(np.float32)
    by_word = np.ascontiguousarray(scaled.reshape(k // 512, 128, 4, n).transpose(0, 1, 3, 2))
    if fmt == "e4m3":
        words = by_word.astype(ml_dtypes.float8_e4m3fn).view(np.uint8)
    else:
        c = by_word.astype(ml_dtypes.float4_e2m1fn).view(np.uint8) & 0xF
        words = (c[..., 0::2] | (c[..., 1::2] << 4)).reshape(k // 512, 128, 2 * n)
    return np.ascontiguousarray(words), np.ascontiguousarray(byte.astype(np.uint8).reshape(k // 512, 16, n))


def unpack_weight(words, scales, fmt):
    g, _, n = scales.shape
    words = np.ascontiguousarray(words).reshape(g, 128, n, -1)
    if fmt == "e4m3":
        vals = words.view(ml_dtypes.float8_e4m3fn).astype(np.float64)
    else:
        nib = np.empty((g, 128, n, 4), np.uint8)
        nib[..., 0::2] = words & 0xF
        nib[..., 1::2] = words >> 4
        vals = E2M1[nib]
    vals = vals * np.repeat(np.exp2(scales.astype(np.float64) - 127.0), 8, axis=1)[..., None]
    return vals.transpose(0, 1, 3, 2).reshape(g * 512, n)


D, E, T, Q, I = 512, 512, 1024, 128, 256


def setup_inputs():
    n = np.random.standard_normal
    idx = np.stack([np.random.permutation(T)[:I] for _ in range(8)])
    fd = mx_kscale(D)
    fe = mx_kscale(E)
    keysp = pack_weight(n((D, T)) / fd[:, None], "e2m1")
    return {
        "query": (n((D, Q)) * 0.6 / np.sqrt(D) * fd[:, None]).astype(np.float32),
        "keys_words": keysp[0],
        "keys_scales": keysp[1],
        "gout": (n((E, Q)) * 1 / np.sqrt(E) * fe[:, None]).astype(np.float32),
        "vals": (n((E, T)) / fe[:, None]).astype(np.float32),
        "zp": (np.random.uniform(200.0, 800.0, (Q, 1))).astype(np.float32),
        "cp": (np.random.uniform(-100.0, 100.0, (Q, 1))).astype(np.float32),
        "dquery": (n((D, Q)) * 1.0 / np.sqrt(D) * fd[:, None]).astype(np.float32),
        "base": (0.5 * n((Q, T))).astype(np.float32),
        "offs": striped8(idx),
    }


def reference(query, keys_words, keys_scales, gout, vals, zp, cp, dquery, base, offs):
    idx = unstriped8(offs)
    keysu = unpack_weight(keys_words, keys_scales, "e2m1")
    queryq = mxq(f64(query), 0, "e4m3")
    a = queryq.T @ keysu
    dqueryq = mxq(f64(dquery), 0, "e4m3")
    ta = dqueryq.T @ keysu
    p = np.exp(pick8(a, idx, 16))
    z = np.sum(p, axis=1, keepdims=True) + f64(zp)
    goutq = mxq(f64(gout), 0, "e4m3")
    valsq = mxq(f64(vals), 0, "e4m3")
    c0 = goutq.T @ valsq
    dz = (np.sum(p * pick8(c0, idx, 16), axis=1, keepdims=True) + f64(cp)) / np.square(z) * (-1.0)
    dp = 1.0 / z * pick8(c0, idx, 16) + dz
    xp = pick8(ta, idx, 16) * p
    xz = np.sum(xp, axis=1, keepdims=True)
    xdz = (np.sum(xp * pick8(c0, idx, 16), axis=1, keepdims=True) - xz * z * 2.0 * (np.sum(p * pick8(c0, idx, 16), axis=1, keepdims=True) + f64(cp)) / np.square(z)) / np.square(z) * (-1.0)
    xdp = xz * 1.0 / np.square(z) * (-1.0) * pick8(c0, idx, 16) + xdz
    xe1 = xdp * p + xp * dp
    xs1 = np.zeros((Q, T))
    xs1[np.arange(Q)[:, None], idx[np.arange(Q) % 128 // 16]] = xe1
    y = xs1 * 1024.0 + f64(base)
    return y

@@ -1,0 +1,185 @@
+from contextlib import ExitStack
+
+import concourse.mybir as mybir
+
+D, E, T, Q, SLOTS = 512, 512, 1024, 128, 256
+FLOPS = 3 * 2 * 512 * 128 * 1024
+
+F32 = mybir.dt.float32
+BF16 = mybir.dt.bfloat16
+I32 = mybir.dt.int32
+U32 = mybir.dt.uint32
+U16 = mybir.dt.uint16
+U8 = mybir.dt.uint8
+FP8X4 = mybir.dt.float8_e4m3fn_x4
+FP4X4 = mybir.dt.float4_e2m1fn_x4
+ALU = mybir.AluOpType
+ACT = mybir.ActivationFunctionType
+
+P = 128
+CHUNKS = (256, 256, 256, 128, 128)
+SCALAR_SHARE = (0, 0, 128, 64, 64)
+COPY_ON_V = (4,)
+STORES = (256, 256, 256, 256)
+
+
+def interleave(copy, grouped, raw, lo, hi):
+    copy(
+        out=grouped[:, lo:hi, :].rearrange("p (c i) t -> p c t i", i=4),
+        in_=raw[:, :, lo:hi].rearrange("p t (c i) -> p c t i", i=4),
+    )
+
+
+def tile_attend_hvsharedprefix_heads_kernel(tc, query, keys_words, keys_scales, gout, vals, zp, cp, dquery, base, offs, out):
+    nc = tc.nc
+    with ExitStack() as ctx:
+        keep = ctx.enter_context(tc.tile_pool(name="keep", bufs=1))
+        psum = ctx.enter_context(tc.psum_pool(name="psum", bufs=1))
+
+        offsets = keep.tile([P, SLOTS // 16], U16, name="offsets")
+        q_raw = keep.tile([P, 4, Q], F32, name="q_raw")
+        dq_raw = keep.tile([P, 4, Q], F32, name="dq_raw")
+        g_raw = keep.tile([P, 4, Q], F32, name="g_raw")
+        k_words = keep.tile([P, 2 * T], U8, name="k_words", align_bytes=64)
+        k_scales = keep.tile([P, T], U8, name="k_scales", align_bytes=64)
+        zp_col = keep.tile([P, 1], F32, name="zp_col")
+        base_sb = keep.tile([P, T], F32, name="base_sb")
+        pc = keep.tile([P, SLOTS + 8], F32, name="pc")
+        tg = keep.tile([P, SLOTS + 8], F32, name="tg")
+        xs = keep.tile([P, T], F32, name="xs")
+        warm = keep.tile([P, 2], F32, name="warm")
+
+        nc.vector.memset(k_scales[:].bitcast(U32), 0)
+        for quad in range(4):
+            nc.scalar.dma_start(
+                out=k_scales[32 * quad : 32 * quad + 4, :].bitcast(I32),
+                in_=keys_scales[0, 4 * quad : 4 * quad + 4, :].bitcast(I32),
+            )
+        nc.gpsimd.memset(warm[:, 0:1], 0.0)
+        nc.scalar.activation(out=warm[:, 1:2], in_=warm[:, 0:1], func=ACT.Exp)
+        nc.gpsimd.memset(xs[:], 0.0)
+        nc.gpsimd.memset(tg[:, SLOTS : SLOTS + 2], 0.0)
+
+        nc.sync.dma_start(out=q_raw[:], in_=query.rearrange("(p j) w -> p j w", j=4))
+        nc.sync.dma_start(out=dq_raw[:], in_=dquery.rearrange("(p j) w -> p j w", j=4))
+        nc.sync.dma_start(out=k_words[:].bitcast(I32), in_=keys_words[0].bitcast(I32))
+        nc.sync.dma_start(out=g_raw[:], in_=gout.rearrange("(p j) w -> p j w", j=4))
+        nc.sync.dma_start(offsets[:], offs)
+        vals_rows = vals.rearrange("(p j) w -> p j w", j=4)
+        v_raw = []
+        start = 0
+        for n, width in enumerate(CHUNKS):
+            raw = keep.tile([P, 4, width], F32, name="v_raw%d" % n)
+            nc.sync.dma_start(out=raw[:], in_=vals_rows[:, :, start : start + width])
+            v_raw.append(raw)
+            start = start + width
+            if n == 1:
+                nc.sync.dma_start(out=zp_col[:], in_=zp)
+                nc.sync.dma_start(out=pc[:, SLOTS : SLOTS + 1], in_=cp)
+        nc.sync.dma_start(out=base_sb[:], in_=base)
+
+        qd_grouped = keep.tile([P, 2 * Q, 4], BF16, name="qd_grouped", align_bytes=64)
+        qd_codes = keep.tile([P, 2 * Q], U32, name="qd_codes", align_bytes=64)
+        qd_scales = keep.tile([P, 2 * Q], U8, name="qd_scales", align_bytes=64)
+        interleave(nc.scalar.copy, qd_grouped[:, 0:Q, :], q_raw, 0, Q)
+        interleave(nc.vector.tensor_copy, qd_grouped[:, Q : 2 * Q, :], dq_raw, 0, Q)
+        nc.vector.quantize_mx(out=qd_codes[:].bitcast(FP8X4), scales=qd_scales[:], in_=qd_grouped[:].rearrange("p w j -> p (w j)"))
+
+        g_grouped = keep.tile([P, Q, 4], BF16, name="g_grouped", align_bytes=64)
+        g_codes = keep.tile([P, Q], U32, name="g_codes", align_bytes=64)
+        g_scales = keep.tile([P, Q], U8, name="g_scales", align_bytes=64)
+        interleave(nc.scalar.copy, g_grouped[:], g_raw, 0, Q)
+        nc.vector.quantize_mx(out=g_codes[:].bitcast(FP8X4), scales=g_scales[:], in_=g_grouped[:].rearrange("p w j -> p (w j)"))
+
+        a_sb = keep.tile([P, T], F32, name="a_sb")
+        ta_sb = keep.tile([P, T], F32, name="ta_sb")
+        c_sb = keep.tile([P, T], F32, name="c_sb")
+
+        def score(which, dest):
+            for half in range(2):
+                bank = psum.tile([P, 512], F32, name="score%d%d" % (which, half))
+                nc.tensor.matmul_mx(
+                    out=bank[:],
+                    lhsT=qd_codes[:, which * Q : (which + 1) * Q].bitcast(FP8X4),
+                    lhsT_scale=qd_scales[:, which * Q : (which + 1) * Q],
+                    rhs=k_words[:, 1024 * half : 1024 * (half + 1)].bitcast(FP4X4),
+                    rhs_scale=k_scales[:, 512 * half : 512 * (half + 1)],
+                    start=True,
+                    stop=True,
+                )
+                nc.scalar.copy(out=dest[:, 512 * half : 512 * (half + 1)], in_=bank[:])
+
+        p = keep.tile([P, SLOTS], F32, name="p")
+        sum_p = keep.tile([P, 1], F32, name="sum_p")
+        score(0, a_sb)
+        nc.scalar.activation(out=p[:], in_=a_sb[:].indirect(offsets[:]), func=ACT.Exp)
+        score(1, ta_sb)
+
+        def value_chunk(n):
+            width = CHUNKS[n]
+            first = sum(CHUNKS[:n])
+            grouped = keep.tile([P, width, 4], BF16, name="v_grouped%d" % n, align_bytes=64)
+            codes = keep.tile([P, width], U32, name="v_codes%d" % n, align_bytes=64)
+            scales = keep.tile([P, width], U8, name="v_scales%d" % n, align_bytes=64)
+            split = width - SCALAR_SHARE[n]
+            if split > 0:
+                interleave(nc.vector.tensor_copy, grouped, v_raw[n], 0, split)
+            if split < width:
+                interleave(nc.scalar.copy, grouped, v_raw[n], split, width)
+            nc.vector.quantize_mx(out=codes[:].bitcast(FP8X4), scales=scales[:], in_=grouped[:].rearrange("p w j -> p (w j)"))
+            bank = psum.tile([P, width], F32, name="c_bank%d" % n, tag=("c_bank%d" % n if n < 4 else "score0%d" % (n - 4)))
+            nc.tensor.matmul_mx(
+                out=bank[:],
+                lhsT=g_codes[:].bitcast(FP8X4),
+                lhsT_scale=g_scales[:],
+                rhs=codes[:].bitcast(FP8X4),
+                rhs_scale=scales[:],
+                start=True,
+                stop=True,
+            )
+            copy = nc.vector.tensor_copy if n in COPY_ON_V else nc.scalar.copy
+            copy(out=c_sb[:, first : first + width], in_=bank[:])
+
+        for n in range(2):
+            value_chunk(n)
+
+        neg_z = keep.tile([P, 1], F32, name="neg_z")
+        neg_r = keep.tile([P, 1], F32, name="neg_r")
+        neg_mean = keep.tile([P, 1], F32, name="neg_mean")
+        scratch = keep.tile([P, SLOTS + 8], F32, name="scratch")
+        scratch2 = keep.tile([P, SLOTS + 8], F32, name="scratch2")
+        centred = keep.tile([P, SLOTS + 8], F32, name="centred")
+        p1 = keep.tile([P, SLOTS], F32, name="p1")
+        p3 = keep.tile([P, SLOTS], F32, name="p3")
+        nc.scalar.activation(out=scratch2[:, 0:SLOTS], in_=p[:], func=ACT.Copy, accum_out=sum_p[:])
+        nc.vector.tensor_scalar(out=neg_z[:], in0=sum_p[:], scalar1=zp_col[:], scalar2=-1.0, op0=ALU.add, op1=ALU.mult)
+        nc.vector.tensor_copy(out=tg[:, 0:SLOTS], in_=ta_sb[:].indirect(offsets[:]))
+        nc.vector.reciprocal(out=neg_r[:], in_=neg_z[:])
+        nc.vector.scalar_tensor_tensor(out=scratch[:, 0:SLOTS], in0=tg[:, 0:SLOTS], scalar=neg_r[:], in1=p[:], op0=ALU.mult, op1=ALU.mult, accum_out=neg_mean[:])
+        nc.scalar.activation(out=p1[:], in_=p[:], func=ACT.Copy, scale=neg_r[:])
+        nc.vector.tensor_scalar(out=centred[:, 0 : SLOTS + 2], in0=tg[:, 0 : SLOTS + 2], scalar1=neg_mean[:], scalar2=neg_r[:], op0=ALU.add, op1=ALU.mult)
+        nc.vector.scalar_tensor_tensor(out=p3[:], in0=p1[:], scalar=-1024.0, in1=centred[:, 0:SLOTS], op0=ALU.mult, op1=ALU.mult)
+
+        for n in range(2, len(CHUNKS)):
+            value_chunk(n)
+
+        x0 = keep.tile([P, SLOTS + 8], F32, name="x0")
+        x1 = keep.tile([P, SLOTS], F32, name="x1")
+        y = keep.tile([P, SLOTS], F32, name="y")
+        total = keep.tile([P, 1], F32, name="total")
+        s1 = keep.tile([P, 1], F32, name="s1")
+        nc.vector.tensor_tensor(out=pc[:, 0:SLOTS], in0=c_sb[:].indirect(offsets[:]), in1=p[:], op=ALU.mult)
+        nc.scalar.activation(out=scratch2[:, 0 : SLOTS + 1], in_=pc[:, 0 : SLOTS + 1], func=ACT.Copy, accum_out=s1[:])
+        nc.vector.scalar_tensor_tensor(out=x0[:, 0 : SLOTS + 1], in0=pc[:, 0 : SLOTS + 1], scalar=-1024.0, in1=centred[:, 0 : SLOTS + 1], op0=ALU.mult, op1=ALU.mult, accum_out=total[:])
+        nc.scalar.activation(out=y[:], in_=p3[:], func=ACT.Copy, scale=s1[:])
+        nc.vector.scalar_tensor_tensor(out=x1[:], in0=p1[:], scalar=total[:], in1=x0[:, 0:SLOTS], op0=ALU.mult, op1=ALU.add)
+        nc.vector.tensor_tensor(out=xs[:].indirect(offsets[:]), in0=x1[:], in1=y[:], op=ALU.add)
+
+        first = 0
+        for n, width in enumerate(STORES):
+            cols = slice(first, first + width)
+            result = keep.tile([P, width], F32, name="result%d" % n)
+            nc.vector.tensor_tensor(out=result[:], in0=xs[:, cols], in1=base_sb[:, cols], op=ALU.add)
+            queue = nc.sync if n % 2 == 0 else nc.scalar
+            queue.dma_start(out=out[:, cols], in_=result[:])
+            first = first + width

@@ -17,10 +17,11 @@ ALU = mybir.AluOpType
 ACT = mybir.ActivationFunctionType
 
 P = 128
-CHUNKS = (256, 256, 256, 128, 128)
-SCALAR_SHARE = (0, 0, 128, 64, 64)
-COPY_ON_V = (4,)
-STORES = (256, 256, 256, 256)
+CHUNKS = (256, 256, 256, 256)
+SCALAR_SHARE = (0, 0, 0, 128)
+COPY_ON_V = ()
+STORES = (320, 256, 256, 192)
+SCORE_COPY_V = ()
 
 
 def interleave(copy, grouped, raw, lo, hi):
@@ -42,135 +43,162 @@ def tile_attend_hvsharedprefix_heads_kernel(tc, query, keys_words, keys_scales, 
         g_raw = keep.tile([P, 4, Q], F32, name="g_raw")
         k_words = keep.tile([P, 2 * T], U8, name="k_words", align_bytes=64)
         k_scales = keep.tile([P, T], U8, name="k_scales", align_bytes=64)
-        zp_col = keep.tile([P, 1], F32, name="zp_col")
+        p = keep.tile([P, SLOTS + 8], F32, name="p")
+        cp_col = keep.tile([P, 1], F32, name="cp_col")
         base_sb = keep.tile([P, T], F32, name="base_sb")
         pc = keep.tile([P, SLOTS + 8], F32, name="pc")
-        tg = keep.tile([P, SLOTS + 8], F32, name="tg")
         xs = keep.tile([P, T], F32, name="xs")
         warm = keep.tile([P, 2], F32, name="warm")
+        v_raw = [keep.tile([P, 4, width], F32, name="v_raw%d" % n, align_bytes=64) for n, width in enumerate(CHUNKS)]
+        vals_rows = vals.rearrange("(p j) w -> p j w", j=4)
 
-        nc.vector.memset(k_scales[:].bitcast(U32), 0)
-        for quad in range(4):
-            nc.scalar.dma_start(
-                out=k_scales[32 * quad : 32 * quad + 4, :].bitcast(I32),
-                in_=keys_scales[0, 4 * quad : 4 * quad + 4, :].bitcast(I32),
-            )
+        def load(what, queue):
+            if what == "s":
+                for quad in range(4):
+                    queue.dma_start(
+                        out=k_scales[32 * quad : 32 * quad + 4, :].bitcast(I32),
+                        in_=keys_scales[0, 4 * quad : 4 * quad + 4, :].bitcast(I32),
+                    )
+            elif what == "q":
+                queue.dma_start(out=q_raw[:], in_=query.rearrange("(p j) w -> p j w", j=4))
+            elif what == "d":
+                queue.dma_start(out=dq_raw[:], in_=dquery.rearrange("(p j) w -> p j w", j=4))
+            elif what == "g":
+                queue.dma_start(out=g_raw[:], in_=gout.rearrange("(p j) w -> p j w", j=4))
+            elif what == "k":
+                queue.dma_start(out=k_words[:].bitcast(I32), in_=keys_words[0].bitcast(I32))
+            elif what == "o":
+                nc.sync.dma_start(offsets[:], offs)
+            elif what == "z":
+                queue.dma_start(out=p[:, SLOTS : SLOTS + 1], in_=zp)
+            elif what == "c":
+                queue.dma_start(out=cp_col[:], in_=cp)
+            elif what == "b":
+                queue.dma_start(out=base_sb[:], in_=base)
+            else:
+                n = int(what)
+                first = sum(CHUNKS[:n])
+                queue.dma_start(out=v_raw[n][:], in_=vals_rows[:, :, first : first + CHUNKS[n]])
+
+        for what in "":
+            load(what, nc.scalar)
+        for what in "":
+            load(what, nc.gpsimd)
         nc.gpsimd.memset(warm[:, 0:1], 0.0)
         nc.scalar.activation(out=warm[:, 1:2], in_=warm[:, 0:1], func=ACT.Exp)
         nc.gpsimd.memset(xs[:], 0.0)
-        nc.gpsimd.memset(tg[:, SLOTS : SLOTS + 2], 0.0)
+        for what in "qskd0oz1gc23b":
+            load(what, nc.sync)
 
-        nc.sync.dma_start(out=q_raw[:], in_=query.rearrange("(p j) w -> p j w", j=4))
-        nc.sync.dma_start(out=dq_raw[:], in_=dquery.rearrange("(p j) w -> p j w", j=4))
-        nc.sync.dma_start(out=k_words[:].bitcast(I32), in_=keys_words[0].bitcast(I32))
-        nc.sync.dma_start(out=g_raw[:], in_=gout.rearrange("(p j) w -> p j w", j=4))
-        nc.sync.dma_start(offsets[:], offs)
-        vals_rows = vals.rearrange("(p j) w -> p j w", j=4)
-        v_raw = []
-        start = 0
-        for n, width in enumerate(CHUNKS):
-            raw = keep.tile([P, 4, width], F32, name="v_raw%d" % n)
-            nc.sync.dma_start(out=raw[:], in_=vals_rows[:, :, start : start + width])
-            v_raw.append(raw)
-            start = start + width
-            if n == 1:
-                nc.sync.dma_start(out=zp_col[:], in_=zp)
-                nc.sync.dma_start(out=pc[:, SLOTS : SLOTS + 1], in_=cp)
-        nc.sync.dma_start(out=base_sb[:], in_=base)
+        def cast_rows(name, raw, width, scalar_share, tag):
+            grouped = keep.tile([P, width, 4], BF16, name=name + "_grouped", tag=tag, align_bytes=64)
+            split = width - scalar_share
+            if split > 0:
+                interleave(nc.vector.tensor_copy, grouped, raw, 0, split)
+            if split < width:
+                interleave(nc.scalar.copy, grouped, raw, split, width)
+            return grouped
 
-        qd_grouped = keep.tile([P, 2 * Q, 4], BF16, name="qd_grouped", align_bytes=64)
-        qd_codes = keep.tile([P, 2 * Q], U32, name="qd_codes", align_bytes=64)
-        qd_scales = keep.tile([P, 2 * Q], U8, name="qd_scales", align_bytes=64)
-        interleave(nc.scalar.copy, qd_grouped[:, 0:Q, :], q_raw, 0, Q)
-        interleave(nc.vector.tensor_copy, qd_grouped[:, Q : 2 * Q, :], dq_raw, 0, Q)
-        nc.vector.quantize_mx(out=qd_codes[:].bitcast(FP8X4), scales=qd_scales[:], in_=qd_grouped[:].rearrange("p w j -> p (w j)"))
+        def quantize(grouped, codes, scales):
+            nc.vector.quantize_mx(out=codes.bitcast(FP8X4), scales=scales, in_=grouped[:].rearrange("p w j -> p (w j)"))
 
-        g_grouped = keep.tile([P, Q, 4], BF16, name="g_grouped", align_bytes=64)
-        g_codes = keep.tile([P, Q], U32, name="g_codes", align_bytes=64)
-        g_scales = keep.tile([P, Q], U8, name="g_scales", align_bytes=64)
-        interleave(nc.scalar.copy, g_grouped[:], g_raw, 0, Q)
-        nc.vector.quantize_mx(out=g_codes[:].bitcast(FP8X4), scales=g_scales[:], in_=g_grouped[:].rearrange("p w j -> p (w j)"))
+        def stationary(name, raw, scalar_share):
+            codes = keep.tile([P, Q], U32, name=name + "_codes", align_bytes=64)
+            scales = keep.tile([P, Q], U8, name=name + "_scales", align_bytes=64)
+            grouped = cast_rows(name, raw, Q, scalar_share, name + "_grouped")
+            return grouped, codes, scales
 
-        a_sb = keep.tile([P, T], F32, name="a_sb")
-        ta_sb = keep.tile([P, T], F32, name="ta_sb")
-        c_sb = keep.tile([P, T], F32, name="c_sb")
+        a_sb = keep.tile([P, T], F32, name="a_sb", align_bytes=64)
 
-        def score(which, dest):
+        def score(which, codes, scales, dest):
             for half in range(2):
                 bank = psum.tile([P, 512], F32, name="score%d%d" % (which, half))
                 nc.tensor.matmul_mx(
                     out=bank[:],
-                    lhsT=qd_codes[:, which * Q : (which + 1) * Q].bitcast(FP8X4),
-                    lhsT_scale=qd_scales[:, which * Q : (which + 1) * Q],
+                    lhsT=codes[:].bitcast(FP8X4),
+                    lhsT_scale=scales[:],
                     rhs=k_words[:, 1024 * half : 1024 * (half + 1)].bitcast(FP4X4),
                     rhs_scale=k_scales[:, 512 * half : 512 * (half + 1)],
                     start=True,
                     stop=True,
                 )
-                nc.scalar.copy(out=dest[:, 512 * half : 512 * (half + 1)], in_=bank[:])
+                copy = nc.vector.tensor_copy if (which, half) in SCORE_COPY_V else nc.scalar.copy
+                copy(out=dest[:, 512 * half : 512 * (half + 1)], in_=bank[:])
 
-        p = keep.tile([P, SLOTS], F32, name="p")
-        sum_p = keep.tile([P, 1], F32, name="sum_p")
-        score(0, a_sb)
-        nc.scalar.activation(out=p[:], in_=a_sb[:].indirect(offsets[:]), func=ACT.Exp)
-        score(1, ta_sb)
+        neg_z = keep.tile([P, 1], F32, name="neg_z")
+        scratch2 = keep.tile([P, SLOTS + 8], F32, name="scratch2")
+        q_grouped, q_codes, q_scales = stationary("q", q_raw, 0)
+        quantize(q_grouped, q_codes[:], q_scales[:])
+        score(0, q_codes, q_scales, a_sb)
+        nc.scalar.activation(out=p[:, 0:SLOTS], in_=a_sb[:].indirect(offsets[:]), func=ACT.Exp)
+        nc.scalar.activation(out=scratch2[:, 0 : SLOTS + 1], in_=p[:, 0 : SLOTS + 1], func=ACT.Copy, scale=-1.0, accum_out=neg_z[:])
+        dq_grouped, dq_codes, dq_scales = stationary("dq", dq_raw, 0)
+        quantize(dq_grouped, dq_codes[:], dq_scales[:])
+        ta_sb = keep.tile([P, T], F32, name="ta_sb", tag="a_sb", align_bytes=64)
+        score(1, dq_codes, dq_scales, ta_sb)
 
-        def value_chunk(n):
-            width = CHUNKS[n]
+        v_codes = keep.tile([P, T], U32, name="v_codes", align_bytes=64)
+        v_scales = keep.tile([P, T], U8, name="v_scales", align_bytes=64)
+
+        def cast_values(n, tag):
+            return cast_rows("v%d" % n, v_raw[n], CHUNKS[n], SCALAR_SHARE[n], tag)
+
+        def quantize_values(n, grouped):
             first = sum(CHUNKS[:n])
-            grouped = keep.tile([P, width, 4], BF16, name="v_grouped%d" % n, align_bytes=64)
-            codes = keep.tile([P, width], U32, name="v_codes%d" % n, align_bytes=64)
-            scales = keep.tile([P, width], U8, name="v_scales%d" % n, align_bytes=64)
-            split = width - SCALAR_SHARE[n]
-            if split > 0:
-                interleave(nc.vector.tensor_copy, grouped, v_raw[n], 0, split)
-            if split < width:
-                interleave(nc.scalar.copy, grouped, v_raw[n], split, width)
-            nc.vector.quantize_mx(out=codes[:].bitcast(FP8X4), scales=scales[:], in_=grouped[:].rearrange("p w j -> p (w j)"))
-            bank = psum.tile([P, width], F32, name="c_bank%d" % n, tag=("c_bank%d" % n if n < 4 else "score0%d" % (n - 4)))
+            quantize(grouped, v_codes[:, first : first + CHUNKS[n]], v_scales[:, first : first + CHUNKS[n]])
+
+        def value_product(first, width):
+            bank = psum.tile([P, width], F32, name="c_bank%d" % first)
             nc.tensor.matmul_mx(
                 out=bank[:],
                 lhsT=g_codes[:].bitcast(FP8X4),
                 lhsT_scale=g_scales[:],
-                rhs=codes[:].bitcast(FP8X4),
-                rhs_scale=scales[:],
+                rhs=v_codes[:, first : first + width].bitcast(FP8X4),
+                rhs_scale=v_scales[:, first : first + width],
                 start=True,
                 stop=True,
             )
-            copy = nc.vector.tensor_copy if n in COPY_ON_V else nc.scalar.copy
-            copy(out=c_sb[:, first : first + width], in_=bank[:])
+            return bank
 
-        for n in range(2):
-            value_chunk(n)
-
-        neg_z = keep.tile([P, 1], F32, name="neg_z")
-        neg_r = keep.tile([P, 1], F32, name="neg_r")
+        grouped0 = cast_values(0, "v0_grouped")
+        quantize_values(0, grouped0)
+        grouped1 = cast_values(1, "v1_grouped")
+        g_grouped, g_codes, g_scales = stationary("g", g_raw, 0)
         neg_mean = keep.tile([P, 1], F32, name="neg_mean")
-        scratch = keep.tile([P, SLOTS + 8], F32, name="scratch")
-        scratch2 = keep.tile([P, SLOTS + 8], F32, name="scratch2")
-        centred = keep.tile([P, SLOTS + 8], F32, name="centred")
         p1 = keep.tile([P, SLOTS], F32, name="p1")
         p3 = keep.tile([P, SLOTS], F32, name="p3")
-        nc.scalar.activation(out=scratch2[:, 0:SLOTS], in_=p[:], func=ACT.Copy, accum_out=sum_p[:])
-        nc.vector.tensor_scalar(out=neg_z[:], in0=sum_p[:], scalar1=zp_col[:], scalar2=-1.0, op0=ALU.add, op1=ALU.mult)
+        quantize_values(1, grouped1)
+        quantize(g_grouped, g_codes[:], g_scales[:])
+        bank01 = value_product(0, 512)
+        grouped2 = cast_values(2, "v2_grouped")
+        tg = keep.tile([P, SLOTS + 16], F32, name="tg", tag="v_raw2", align_bytes=64)
+        nc.gpsimd.memset(tg[:, SLOTS : SLOTS + 1], 0.0)
+        neg_r = tg[:, SLOTS + 8 : SLOTS + 9]
+        nc.vector.reciprocal(out=neg_r, in_=neg_z[:])
+        nc.scalar.activation(out=p1[:], in_=p[:, 0:SLOTS], func=ACT.Copy, scale=neg_r)
+        nc.scalar.activation(out=pc[:, SLOTS : SLOTS + 1], in_=cp_col[:], func=ACT.Copy, scale=neg_r)
+        quantize_values(2, grouped2)
+        bank2 = value_product(512, 256)
+        grouped3 = cast_values(3, "v3_grouped")
         nc.vector.tensor_copy(out=tg[:, 0:SLOTS], in_=ta_sb[:].indirect(offsets[:]))
-        nc.vector.reciprocal(out=neg_r[:], in_=neg_z[:])
-        nc.vector.scalar_tensor_tensor(out=scratch[:, 0:SLOTS], in0=tg[:, 0:SLOTS], scalar=neg_r[:], in1=p[:], op0=ALU.mult, op1=ALU.mult, accum_out=neg_mean[:])
-        nc.scalar.activation(out=p1[:], in_=p[:], func=ACT.Copy, scale=neg_r[:])
-        nc.vector.tensor_scalar(out=centred[:, 0 : SLOTS + 2], in0=tg[:, 0 : SLOTS + 2], scalar1=neg_mean[:], scalar2=neg_r[:], op0=ALU.add, op1=ALU.mult)
-        nc.vector.scalar_tensor_tensor(out=p3[:], in0=p1[:], scalar=-1024.0, in1=centred[:, 0:SLOTS], op0=ALU.mult, op1=ALU.mult)
-
-        for n in range(2, len(CHUNKS)):
-            value_chunk(n)
+        quantize_values(3, grouped3)
+        bank3 = value_product(768, 256)
+        scratch = keep.tile([P, SLOTS + 8], F32, name="scratch", tag="v3_grouped", align_bytes=64)
+        nc.vector.scalar_tensor_tensor(out=scratch[:, 0:SLOTS], in0=tg[:, 0:SLOTS], scalar=neg_r, in1=p[:, 0:SLOTS], op0=ALU.mult, op1=ALU.mult, accum_out=neg_mean[:])
+        nc.vector.scalar_tensor_tensor(out=p3[:], in0=p1[:], scalar=neg_mean[:], in1=scratch[:, 0:SLOTS], op0=ALU.mult, op1=ALU.add)
+        c_sb = keep.tile([P, T], F32, name="c_sb", tag="v_raw3", align_bytes=64)
+        nc.scalar.copy(out=c_sb[:, 0:512], in_=bank01[:])
+        nc.scalar.copy(out=c_sb[:, 512:768], in_=bank2[:])
+        nc.scalar.copy(out=c_sb[:, 768:1024], in_=bank3[:])
 
         x0 = keep.tile([P, SLOTS + 8], F32, name="x0")
         x1 = keep.tile([P, SLOTS], F32, name="x1")
         y = keep.tile([P, SLOTS], F32, name="y")
         total = keep.tile([P, 1], F32, name="total")
         s1 = keep.tile([P, 1], F32, name="s1")
-        nc.vector.tensor_tensor(out=pc[:, 0:SLOTS], in0=c_sb[:].indirect(offsets[:]), in1=p[:], op=ALU.mult)
+        nc.vector.tensor_tensor(out=pc[:, 0:SLOTS], in0=c_sb[:].indirect(offsets[:]), in1=p1[:], op=ALU.mult)
         nc.scalar.activation(out=scratch2[:, 0 : SLOTS + 1], in_=pc[:, 0 : SLOTS + 1], func=ACT.Copy, accum_out=s1[:])
-        nc.vector.scalar_tensor_tensor(out=x0[:, 0 : SLOTS + 1], in0=pc[:, 0 : SLOTS + 1], scalar=-1024.0, in1=centred[:, 0 : SLOTS + 1], op0=ALU.mult, op1=ALU.mult, accum_out=total[:])
+        nc.vector.scalar_tensor_tensor(out=x0[:, 0 : SLOTS + 1], in0=tg[:, 0 : SLOTS + 1], scalar=neg_mean[:], in1=pc[:, 0 : SLOTS + 1], op0=ALU.add, op1=ALU.mult, accum_out=total[:])
         nc.scalar.activation(out=y[:], in_=p3[:], func=ACT.Copy, scale=s1[:])
         nc.vector.scalar_tensor_tensor(out=x1[:], in0=p1[:], scalar=total[:], in1=x0[:, 0:SLOTS], op0=ALU.mult, op1=ALU.add)
         nc.vector.tensor_tensor(out=xs[:].indirect(offsets[:]), in0=x1[:], in1=y[:], op=ALU.add)
@@ -179,7 +207,7 @@ def tile_attend_hvsharedprefix_heads_kernel(tc, query, keys_words, keys_scales, 
         for n, width in enumerate(STORES):
             cols = slice(first, first + width)
             result = keep.tile([P, width], F32, name="result%d" % n)
-            nc.vector.tensor_tensor(out=result[:], in0=xs[:, cols], in1=base_sb[:, cols], op=ALU.add)
+            nc.vector.scalar_tensor_tensor(out=result[:], in0=xs[:, cols], scalar=-1024.0, in1=base_sb[:, cols], op0=ALU.mult, op1=ALU.add)
             queue = nc.sync if n % 2 == 0 else nc.scalar
             queue.dma_start(out=out[:, cols], in_=result[:])
             first = first + width

@@ -2,8 +2,8 @@ from contextlib import ExitStack
 
 import concourse.mybir as mybir
 
-D, E, T, Q, SLOTS = 512, 512, 1024, 128, 256
-FLOPS = 3 * 2 * 512 * 128 * 1024
+T, Q, SLOTS = 1024, 128, 256
+FLOPS = 3 * 2 * 512 * Q * T
 
 F32 = mybir.dt.float32
 BF16 = mybir.dt.bfloat16
@@ -17,18 +17,25 @@ ALU = mybir.AluOpType
 ACT = mybir.ActivationFunctionType
 
 P = 128
-CHUNKS = (256, 256, 256, 256)
-SCALAR_SHARE = (0, 0, 0, 128)
-COPY_ON_V = ()
-STORES = (320, 256, 256, 192)
-SCORE_COPY_V = ()
+PACK = 4
+BANK = 512
+CHUNK = 256
+CHUNKS = T // CHUNK
+LINE = 8
+OUT_SCALE = 1024.0
+LAST_CHUNK_ON_SCALAR = 128
+OUT_PIECES = (320, 256, 256, 192)
 
 
-def interleave(copy, grouped, raw, lo, hi):
+def interleave(copy, grouped, raw, first, last):
     copy(
-        out=grouped[:, lo:hi, :].rearrange("p (c i) t -> p c t i", i=4),
-        in_=raw[:, :, lo:hi].rearrange("p t (c i) -> p c t i", i=4),
+        out=grouped[:, first:last, :].rearrange("p (c i) t -> p c t i", i=4),
+        in_=raw[:, :, first:last].rearrange("p t (c i) -> p c t i", i=4),
     )
+
+
+def by_partition(rows):
+    return rows.rearrange("(p t) w -> p t w", t=PACK)
 
 
 def tile_attend_hvsharedprefix_heads_kernel(tc, query, keys_words, keys_scales, gout, vals, zp, cp, dquery, base, offs, out):
@@ -38,176 +45,167 @@ def tile_attend_hvsharedprefix_heads_kernel(tc, query, keys_words, keys_scales, 
         psum = ctx.enter_context(tc.psum_pool(name="psum", bufs=1))
 
         offsets = keep.tile([P, SLOTS // 16], U16, name="offsets")
-        q_raw = keep.tile([P, 4, Q], F32, name="q_raw")
-        dq_raw = keep.tile([P, 4, Q], F32, name="dq_raw")
-        g_raw = keep.tile([P, 4, Q], F32, name="g_raw")
+        q_raw = keep.tile([P, PACK, Q], F32, name="q_raw")
+        dq_raw = keep.tile([P, PACK, Q], F32, name="dq_raw")
+        g_raw = keep.tile([P, PACK, Q], F32, name="g_raw")
         k_words = keep.tile([P, 2 * T], U8, name="k_words", align_bytes=64)
         k_scales = keep.tile([P, T], U8, name="k_scales", align_bytes=64)
-        p = keep.tile([P, SLOTS + 8], F32, name="p")
+        p = keep.tile([P, SLOTS + LINE], F32, name="p")
         cp_col = keep.tile([P, 1], F32, name="cp_col")
         base_sb = keep.tile([P, T], F32, name="base_sb")
-        pc = keep.tile([P, SLOTS + 8], F32, name="pc")
-        xs = keep.tile([P, T], F32, name="xs")
-        warm = keep.tile([P, 2], F32, name="warm")
-        v_raw = [keep.tile([P, 4, width], F32, name="v_raw%d" % n, align_bytes=64) for n, width in enumerate(CHUNKS)]
-        vals_rows = vals.rearrange("(p j) w -> p j w", j=4)
+        pc = keep.tile([P, SLOTS + LINE], F32, name="pc")
+        placed = keep.tile([P, T], F32, name="placed")
+        v_raw = [keep.tile([P, PACK, CHUNK], F32, name="v_raw%d" % n, align_bytes=64) for n in range(CHUNKS)]
 
-        def load(what, queue):
-            if what == "s":
-                for quad in range(4):
-                    queue.dma_start(
-                        out=k_scales[32 * quad : 32 * quad + 4, :].bitcast(I32),
-                        in_=keys_scales[0, 4 * quad : 4 * quad + 4, :].bitcast(I32),
-                    )
-            elif what == "q":
-                queue.dma_start(out=q_raw[:], in_=query.rearrange("(p j) w -> p j w", j=4))
-            elif what == "d":
-                queue.dma_start(out=dq_raw[:], in_=dquery.rearrange("(p j) w -> p j w", j=4))
-            elif what == "g":
-                queue.dma_start(out=g_raw[:], in_=gout.rearrange("(p j) w -> p j w", j=4))
-            elif what == "k":
-                queue.dma_start(out=k_words[:].bitcast(I32), in_=keys_words[0].bitcast(I32))
-            elif what == "o":
-                nc.sync.dma_start(offsets[:], offs)
-            elif what == "z":
-                queue.dma_start(out=p[:, SLOTS : SLOTS + 1], in_=zp)
-            elif what == "c":
-                queue.dma_start(out=cp_col[:], in_=cp)
-            elif what == "b":
-                queue.dma_start(out=base_sb[:], in_=base)
-            else:
-                n = int(what)
-                first = sum(CHUNKS[:n])
-                queue.dma_start(out=v_raw[n][:], in_=vals_rows[:, :, first : first + CHUNKS[n]])
+        def load_values(n):
+            nc.sync.dma_start(out=v_raw[n][:], in_=by_partition(vals)[:, :, n * CHUNK : (n + 1) * CHUNK])
 
-        for what in "":
-            load(what, nc.scalar)
-        for what in "":
-            load(what, nc.gpsimd)
-        nc.gpsimd.memset(warm[:, 0:1], 0.0)
-        nc.scalar.activation(out=warm[:, 1:2], in_=warm[:, 0:1], func=ACT.Exp)
-        nc.gpsimd.memset(xs[:], 0.0)
-        for what in "qskd0oz1gc23b":
-            load(what, nc.sync)
+        nc.gpsimd.memset(placed[:], 0.0)
 
-        def cast_rows(name, raw, width, scalar_share, tag):
-            grouped = keep.tile([P, width, 4], BF16, name=name + "_grouped", tag=tag, align_bytes=64)
-            split = width - scalar_share
-            if split > 0:
-                interleave(nc.vector.tensor_copy, grouped, raw, 0, split)
-            if split < width:
-                interleave(nc.scalar.copy, grouped, raw, split, width)
+        nc.sync.dma_start(out=q_raw[:], in_=by_partition(query))
+        for quadrant in range(4):
+            nc.sync.dma_start(
+                out=k_scales[32 * quadrant : 32 * quadrant + 4, :].bitcast(I32),
+                in_=keys_scales[0, 4 * quadrant : 4 * quadrant + 4, :].bitcast(I32),
+            )
+        nc.sync.dma_start(out=k_words[:].bitcast(I32), in_=keys_words[0].bitcast(I32))
+        nc.sync.dma_start(out=dq_raw[:], in_=by_partition(dquery))
+        load_values(0)
+        nc.sync.dma_start(offsets[:], offs)
+        nc.sync.dma_start(out=p[:, SLOTS : SLOTS + 1], in_=zp)
+        load_values(1)
+        nc.sync.dma_start(out=g_raw[:], in_=by_partition(gout))
+        load_values(2)
+        load_values(3)
+        nc.sync.dma_start(out=cp_col[:], in_=cp)
+        nc.sync.dma_start(out=base_sb[:], in_=base)
+
+        def round_rows(name, raw, width, on_scalar):
+            grouped = keep.tile([P, width, PACK], BF16, name=name + "_grouped", align_bytes=64)
+            interleave(nc.vector.tensor_copy, grouped, raw, 0, width - on_scalar)
+            if on_scalar:
+                interleave(nc.scalar.copy, grouped, raw, width - on_scalar, width)
             return grouped
 
         def quantize(grouped, codes, scales):
-            nc.vector.quantize_mx(out=codes.bitcast(FP8X4), scales=scales, in_=grouped[:].rearrange("p w j -> p (w j)"))
+            nc.vector.quantize_mx(out=codes.bitcast(FP8X4), scales=scales, in_=grouped[:].rearrange("p w t -> p (w t)"))
 
-        def stationary(name, raw, scalar_share):
+        def row_operand(name, raw):
             codes = keep.tile([P, Q], U32, name=name + "_codes", align_bytes=64)
             scales = keep.tile([P, Q], U8, name=name + "_scales", align_bytes=64)
-            grouped = cast_rows(name, raw, Q, scalar_share, name + "_grouped")
-            return grouped, codes, scales
+            return round_rows(name, raw, Q, 0), codes, scales
 
-        a_sb = keep.tile([P, T], F32, name="a_sb", align_bytes=64)
-
-        def score(which, codes, scales, dest):
-            for half in range(2):
-                bank = psum.tile([P, 512], F32, name="score%d%d" % (which, half))
+        def score_keys(name, codes, scales, scores):
+            for half in range(T // BANK):
+                tokens = slice(BANK * half, BANK * (half + 1))
+                bank = psum.tile([P, BANK], F32, name="%s_bank%d" % (name, half))
                 nc.tensor.matmul_mx(
                     out=bank[:],
                     lhsT=codes[:].bitcast(FP8X4),
                     lhsT_scale=scales[:],
-                    rhs=k_words[:, 1024 * half : 1024 * (half + 1)].bitcast(FP4X4),
-                    rhs_scale=k_scales[:, 512 * half : 512 * (half + 1)],
+                    rhs=k_words[:, 2 * tokens.start : 2 * tokens.stop].bitcast(FP4X4),
+                    rhs_scale=k_scales[:, tokens],
                     start=True,
                     stop=True,
                 )
-                copy = nc.vector.tensor_copy if (which, half) in SCORE_COPY_V else nc.scalar.copy
-                copy(out=dest[:, 512 * half : 512 * (half + 1)], in_=bank[:])
+                nc.scalar.activation(out=scores[:, tokens], in_=bank[:], func=ACT.Copy)
 
+        a_sb = keep.tile([P, T], F32, name="a_sb", align_bytes=64)
         neg_z = keep.tile([P, 1], F32, name="neg_z")
-        scratch2 = keep.tile([P, SLOTS + 8], F32, name="scratch2")
-        q_grouped, q_codes, q_scales = stationary("q", q_raw, 0)
+        summed = keep.tile([P, SLOTS + LINE], F32, name="summed")
+        q_grouped, q_codes, q_scales = row_operand("q", q_raw)
         quantize(q_grouped, q_codes[:], q_scales[:])
-        score(0, q_codes, q_scales, a_sb)
+        score_keys("a", q_codes, q_scales, a_sb)
         nc.scalar.activation(out=p[:, 0:SLOTS], in_=a_sb[:].indirect(offsets[:]), func=ACT.Exp)
-        nc.scalar.activation(out=scratch2[:, 0 : SLOTS + 1], in_=p[:, 0 : SLOTS + 1], func=ACT.Copy, scale=-1.0, accum_out=neg_z[:])
-        dq_grouped, dq_codes, dq_scales = stationary("dq", dq_raw, 0)
+        nc.scalar.activation(out=summed[:, 0 : SLOTS + 1], in_=p[:, 0 : SLOTS + 1], func=ACT.Copy, scale=-1.0, accum_out=neg_z[:])
+        dq_grouped, dq_codes, dq_scales = row_operand("dq", dq_raw)
         quantize(dq_grouped, dq_codes[:], dq_scales[:])
         ta_sb = keep.tile([P, T], F32, name="ta_sb", tag="a_sb", align_bytes=64)
-        score(1, dq_codes, dq_scales, ta_sb)
+        score_keys("ta", dq_codes, dq_scales, ta_sb)
 
         v_codes = keep.tile([P, T], U32, name="v_codes", align_bytes=64)
         v_scales = keep.tile([P, T], U8, name="v_scales", align_bytes=64)
 
-        def cast_values(n, tag):
-            return cast_rows("v%d" % n, v_raw[n], CHUNKS[n], SCALAR_SHARE[n], tag)
+        def round_values(n):
+            return round_rows("v%d" % n, v_raw[n], CHUNK, LAST_CHUNK_ON_SCALAR if n == CHUNKS - 1 else 0)
 
         def quantize_values(n, grouped):
-            first = sum(CHUNKS[:n])
-            quantize(grouped, v_codes[:, first : first + CHUNKS[n]], v_scales[:, first : first + CHUNKS[n]])
+            tokens = slice(n * CHUNK, (n + 1) * CHUNK)
+            quantize(grouped, v_codes[:, tokens], v_scales[:, tokens])
 
-        def value_product(first, width):
-            bank = psum.tile([P, width], F32, name="c_bank%d" % first)
+        def score_values(tokens):
+            bank = psum.tile([P, tokens.stop - tokens.start], F32, name="c_bank%d" % tokens.start)
             nc.tensor.matmul_mx(
                 out=bank[:],
                 lhsT=g_codes[:].bitcast(FP8X4),
                 lhsT_scale=g_scales[:],
-                rhs=v_codes[:, first : first + width].bitcast(FP8X4),
-                rhs_scale=v_scales[:, first : first + width],
+                rhs=v_codes[:, tokens].bitcast(FP8X4),
+                rhs_scale=v_scales[:, tokens],
                 start=True,
                 stop=True,
             )
             return bank
 
-        grouped0 = cast_values(0, "v0_grouped")
-        quantize_values(0, grouped0)
-        grouped1 = cast_values(1, "v1_grouped")
-        g_grouped, g_codes, g_scales = stationary("g", g_raw, 0)
-        neg_mean = keep.tile([P, 1], F32, name="neg_mean")
-        p1 = keep.tile([P, SLOTS], F32, name="p1")
-        p3 = keep.tile([P, SLOTS], F32, name="p3")
-        quantize_values(1, grouped1)
+        c_parts = (slice(0, 2 * CHUNK), slice(2 * CHUNK, 3 * CHUNK), slice(3 * CHUNK, 4 * CHUNK))
+        quantize_values(0, round_values(0))
+        v1_grouped = round_values(1)
+        g_grouped, g_codes, g_scales = row_operand("g", g_raw)
+        neg_m = keep.tile([P, 1], F32, name="neg_m")
+        rp = keep.tile([P, SLOTS], F32, name="rp")
+        rp_centred = keep.tile([P, SLOTS], F32, name="rp_centred")
+        quantize_values(1, v1_grouped)
         quantize(g_grouped, g_codes[:], g_scales[:])
-        bank01 = value_product(0, 512)
-        grouped2 = cast_values(2, "v2_grouped")
-        tg = keep.tile([P, SLOTS + 16], F32, name="tg", tag="v_raw2", align_bytes=64)
-        nc.gpsimd.memset(tg[:, SLOTS : SLOTS + 1], 0.0)
-        neg_r = tg[:, SLOTS + 8 : SLOTS + 9]
-        nc.vector.reciprocal(out=neg_r, in_=neg_z[:])
-        nc.scalar.activation(out=p1[:], in_=p[:, 0:SLOTS], func=ACT.Copy, scale=neg_r)
-        nc.scalar.activation(out=pc[:, SLOTS : SLOTS + 1], in_=cp_col[:], func=ACT.Copy, scale=neg_r)
-        quantize_values(2, grouped2)
-        bank2 = value_product(512, 256)
-        grouped3 = cast_values(3, "v3_grouped")
-        nc.vector.tensor_copy(out=tg[:, 0:SLOTS], in_=ta_sb[:].indirect(offsets[:]))
-        quantize_values(3, grouped3)
-        bank3 = value_product(768, 256)
-        scratch = keep.tile([P, SLOTS + 8], F32, name="scratch", tag="v3_grouped", align_bytes=64)
-        nc.vector.scalar_tensor_tensor(out=scratch[:, 0:SLOTS], in0=tg[:, 0:SLOTS], scalar=neg_r, in1=p[:, 0:SLOTS], op0=ALU.mult, op1=ALU.mult, accum_out=neg_mean[:])
-        nc.vector.scalar_tensor_tensor(out=p3[:], in0=p1[:], scalar=neg_mean[:], in1=scratch[:, 0:SLOTS], op0=ALU.mult, op1=ALU.add)
-        c_sb = keep.tile([P, T], F32, name="c_sb", tag="v_raw3", align_bytes=64)
-        nc.scalar.copy(out=c_sb[:, 0:512], in_=bank01[:])
-        nc.scalar.copy(out=c_sb[:, 512:768], in_=bank2[:])
-        nc.scalar.copy(out=c_sb[:, 768:1024], in_=bank3[:])
+        c_banks = [score_values(c_parts[0])]
+        v2_grouped = round_values(2)
 
-        x0 = keep.tile([P, SLOTS + 8], F32, name="x0")
-        x1 = keep.tile([P, SLOTS], F32, name="x1")
-        y = keep.tile([P, SLOTS], F32, name="y")
-        total = keep.tile([P, 1], F32, name="total")
-        s1 = keep.tile([P, 1], F32, name="s1")
-        nc.vector.tensor_tensor(out=pc[:, 0:SLOTS], in0=c_sb[:].indirect(offsets[:]), in1=p1[:], op=ALU.mult)
-        nc.scalar.activation(out=scratch2[:, 0 : SLOTS + 1], in_=pc[:, 0 : SLOTS + 1], func=ACT.Copy, accum_out=s1[:])
-        nc.vector.scalar_tensor_tensor(out=x0[:, 0 : SLOTS + 1], in0=tg[:, 0 : SLOTS + 1], scalar=neg_mean[:], in1=pc[:, 0 : SLOTS + 1], op0=ALU.add, op1=ALU.mult, accum_out=total[:])
-        nc.scalar.activation(out=y[:], in_=p3[:], func=ACT.Copy, scale=s1[:])
-        nc.vector.scalar_tensor_tensor(out=x1[:], in0=p1[:], scalar=total[:], in1=x0[:, 0:SLOTS], op0=ALU.mult, op1=ALU.add)
-        nc.vector.tensor_tensor(out=xs[:].indirect(offsets[:]), in0=x1[:], in1=y[:], op=ALU.add)
+        t_slots = keep.tile([P, SLOTS + 2 * LINE], F32, name="t_slots", tag="v_raw2", align_bytes=64)
+        nc.gpsimd.memset(t_slots[:, SLOTS : SLOTS + 1], 0.0)
+        neg_r = t_slots[:, SLOTS + LINE : SLOTS + LINE + 1]
+        nc.vector.reciprocal(out=neg_r, in_=neg_z[:])
+        nc.scalar.activation(out=rp[:], in_=p[:, 0:SLOTS], func=ACT.Copy, scale=neg_r)
+        quantize_values(2, v2_grouped)
+        c_banks.append(score_values(c_parts[1]))
+        v3_grouped = round_values(3)
+        nc.vector.tensor_copy(out=t_slots[:, 0:SLOTS], in_=ta_sb[:].indirect(offsets[:]))
+        quantize_values(3, v3_grouped)
+        c_banks.append(score_values(c_parts[2]))
+
+        rpt = keep.tile([P, SLOTS + LINE], F32, name="rpt", tag="v3_grouped", align_bytes=64)
+        nc.vector.scalar_tensor_tensor(
+            out=rpt[:, 0:SLOTS], in0=t_slots[:, 0:SLOTS], scalar=neg_r, in1=p[:, 0:SLOTS], op0=ALU.mult, op1=ALU.mult, accum_out=neg_m[:]
+        )
+        nc.vector.scalar_tensor_tensor(out=rp_centred[:], in0=rp[:], scalar=neg_m[:], in1=rpt[:, 0:SLOTS], op0=ALU.mult, op1=ALU.add)
+
+        c_sb = keep.tile([P, T], F32, name="c_sb", tag="v_raw3", align_bytes=64)
+        for tokens, bank in zip(c_parts, c_banks):
+            nc.scalar.copy(out=c_sb[:, tokens], in_=bank[:])
+        nc.scalar.activation(out=pc[:, SLOTS : SLOTS + 1], in_=cp_col[:], func=ACT.Copy, scale=neg_r)
+
+        term1 = keep.tile([P, SLOTS + LINE], F32, name="term1")
+        terms12 = keep.tile([P, SLOTS], F32, name="terms12")
+        term3 = keep.tile([P, SLOTS], F32, name="term3")
+        term1_sum = keep.tile([P, 1], F32, name="term1_sum")
+        pc_sum = keep.tile([P, 1], F32, name="pc_sum")
+        nc.vector.tensor_tensor(out=pc[:, 0:SLOTS], in0=c_sb[:].indirect(offsets[:]), in1=rp[:], op=ALU.mult)
+        nc.scalar.activation(out=summed[:, 0 : SLOTS + 1], in_=pc[:, 0 : SLOTS + 1], func=ACT.Copy, accum_out=pc_sum[:])
+        nc.vector.scalar_tensor_tensor(
+            out=term1[:, 0 : SLOTS + 1],
+            in0=t_slots[:, 0 : SLOTS + 1],
+            scalar=neg_m[:],
+            in1=pc[:, 0 : SLOTS + 1],
+            op0=ALU.add,
+            op1=ALU.mult,
+            accum_out=term1_sum[:],
+        )
+        nc.scalar.activation(out=term3[:], in_=rp_centred[:], func=ACT.Copy, scale=pc_sum[:])
+        nc.vector.scalar_tensor_tensor(out=terms12[:], in0=rp[:], scalar=term1_sum[:], in1=term1[:, 0:SLOTS], op0=ALU.mult, op1=ALU.add)
+        nc.vector.tensor_tensor(out=placed[:].indirect(offsets[:]), in0=terms12[:], in1=term3[:], op=ALU.add)
 
         first = 0
-        for n, width in enumerate(STORES):
+        for n, width in enumerate(OUT_PIECES):
             cols = slice(first, first + width)
             result = keep.tile([P, width], F32, name="result%d" % n)
-            nc.vector.scalar_tensor_tensor(out=result[:], in0=xs[:, cols], scalar=-1024.0, in1=base_sb[:, cols], op0=ALU.mult, op1=ALU.add)
+            nc.vector.scalar_tensor_tensor(out=result[:], in0=placed[:, cols], scalar=-OUT_SCALE, in1=base_sb[:, cols], op0=ALU.mult, op1=ALU.add)
             queue = nc.sync if n % 2 == 0 else nc.scalar
             queue.dma_start(out=out[:, cols], in_=result[:])
             first = first + width

from contextlib import ExitStack

import concourse.mybir as mybir

T, Q, SLOTS = 1024, 128, 256
FLOPS = 3 * 2 * 512 * Q * T

F32 = mybir.dt.float32
BF16 = mybir.dt.bfloat16
I32 = mybir.dt.int32
U32 = mybir.dt.uint32
U16 = mybir.dt.uint16
U8 = mybir.dt.uint8
FP8X4 = mybir.dt.float8_e4m3fn_x4
FP4X4 = mybir.dt.float4_e2m1fn_x4
ALU = mybir.AluOpType
ACT = mybir.ActivationFunctionType

P = 128
PACK = 4
BANK = 512
CHUNK = 256
CHUNKS = T // CHUNK
LINE = 8
OUT_SCALE = 1024.0
LAST_CHUNK_ON_SCALAR = 128
OUT_PIECES = (320, 256, 256, 192)


def interleave(copy, grouped, raw, first, last):
    copy(
        out=grouped[:, first:last, :].rearrange("p (c i) t -> p c t i", i=4),
        in_=raw[:, :, first:last].rearrange("p t (c i) -> p c t i", i=4),
    )


def by_partition(rows):
    return rows.rearrange("(p t) w -> p t w", t=PACK)


def tile_attend_hvsharedprefix_heads_kernel(tc, query, keys_words, keys_scales, gout, vals, zp, cp, dquery, base, offs, out):
    nc = tc.nc
    with ExitStack() as ctx:
        keep = ctx.enter_context(tc.tile_pool(name="keep", bufs=1))
        psum = ctx.enter_context(tc.psum_pool(name="psum", bufs=1))

        offsets = keep.tile([P, SLOTS // 16], U16, name="offsets")
        q_raw = keep.tile([P, PACK, Q], F32, name="q_raw")
        dq_raw = keep.tile([P, PACK, Q], F32, name="dq_raw")
        g_raw = keep.tile([P, PACK, Q], F32, name="g_raw")
        k_words = keep.tile([P, 2 * T], U8, name="k_words", align_bytes=64)
        k_scales = keep.tile([P, T], U8, name="k_scales", align_bytes=64)
        p = keep.tile([P, SLOTS + LINE], F32, name="p")
        cp_col = keep.tile([P, 1], F32, name="cp_col")
        base_sb = keep.tile([P, T], F32, name="base_sb")
        pc = keep.tile([P, SLOTS + LINE], F32, name="pc")
        placed = keep.tile([P, T], F32, name="placed")
        v_raw = [keep.tile([P, PACK, CHUNK], F32, name="v_raw%d" % n, align_bytes=64) for n in range(CHUNKS)]

        def load_values(n):
            nc.sync.dma_start(out=v_raw[n][:], in_=by_partition(vals)[:, :, n * CHUNK : (n + 1) * CHUNK])

        nc.gpsimd.memset(placed[:], 0.0)

        nc.sync.dma_start(out=q_raw[:], in_=by_partition(query))
        for quadrant in range(4):
            nc.sync.dma_start(
                out=k_scales[32 * quadrant : 32 * quadrant + 4, :].bitcast(I32),
                in_=keys_scales[0, 4 * quadrant : 4 * quadrant + 4, :].bitcast(I32),
            )
        nc.sync.dma_start(out=k_words[:].bitcast(I32), in_=keys_words[0].bitcast(I32))
        nc.sync.dma_start(out=dq_raw[:], in_=by_partition(dquery))
        load_values(0)
        nc.sync.dma_start(offsets[:], offs)
        nc.sync.dma_start(out=p[:, SLOTS : SLOTS + 1], in_=zp)
        load_values(1)
        nc.sync.dma_start(out=g_raw[:], in_=by_partition(gout))
        load_values(2)
        load_values(3)
        nc.sync.dma_start(out=cp_col[:], in_=cp)
        nc.sync.dma_start(out=base_sb[:], in_=base)

        def round_rows(name, raw, width, on_scalar):
            grouped = keep.tile([P, width, PACK], BF16, name=name + "_grouped", align_bytes=64)
            interleave(nc.vector.tensor_copy, grouped, raw, 0, width - on_scalar)
            if on_scalar:
                interleave(nc.scalar.copy, grouped, raw, width - on_scalar, width)
            return grouped

        def quantize(grouped, codes, scales):
            nc.vector.quantize_mx(out=codes.bitcast(FP8X4), scales=scales, in_=grouped[:].rearrange("p w t -> p (w t)"))

        def row_operand(name, raw):
            codes = keep.tile([P, Q], U32, name=name + "_codes", align_bytes=64)
            scales = keep.tile([P, Q], U8, name=name + "_scales", align_bytes=64)
            return round_rows(name, raw, Q, 0), codes, scales

        def score_keys(name, codes, scales, scores):
            for half in range(T // BANK):
                tokens = slice(BANK * half, BANK * (half + 1))
                bank = psum.tile([P, BANK], F32, name="%s_bank%d" % (name, half))
                nc.tensor.matmul_mx(
                    out=bank[:],
                    lhsT=codes[:].bitcast(FP8X4),
                    lhsT_scale=scales[:],
                    rhs=k_words[:, 2 * tokens.start : 2 * tokens.stop].bitcast(FP4X4),
                    rhs_scale=k_scales[:, tokens],
                    start=True,
                    stop=True,
                )
                nc.scalar.activation(out=scores[:, tokens], in_=bank[:], func=ACT.Copy)

        a_sb = keep.tile([P, T], F32, name="a_sb", align_bytes=64)
        neg_z = keep.tile([P, 1], F32, name="neg_z")
        summed = keep.tile([P, SLOTS + LINE], F32, name="summed")
        q_grouped, q_codes, q_scales = row_operand("q", q_raw)
        quantize(q_grouped, q_codes[:], q_scales[:])
        score_keys("a", q_codes, q_scales, a_sb)
        nc.scalar.activation(out=p[:, 0:SLOTS], in_=a_sb[:].indirect(offsets[:]), func=ACT.Exp)
        nc.scalar.activation(out=summed[:, 0 : SLOTS + 1], in_=p[:, 0 : SLOTS + 1], func=ACT.Copy, scale=-1.0, accum_out=neg_z[:])
        dq_grouped, dq_codes, dq_scales = row_operand("dq", dq_raw)
        quantize(dq_grouped, dq_codes[:], dq_scales[:])
        ta_sb = keep.tile([P, T], F32, name="ta_sb", tag="a_sb", align_bytes=64)
        score_keys("ta", dq_codes, dq_scales, ta_sb)

        v_codes = keep.tile([P, T], U32, name="v_codes", align_bytes=64)
        v_scales = keep.tile([P, T], U8, name="v_scales", align_bytes=64)

        def round_values(n):
            return round_rows("v%d" % n, v_raw[n], CHUNK, LAST_CHUNK_ON_SCALAR if n == CHUNKS - 1 else 0)

        def quantize_values(n, grouped):
            tokens = slice(n * CHUNK, (n + 1) * CHUNK)
            quantize(grouped, v_codes[:, tokens], v_scales[:, tokens])

        def score_values(tokens):
            bank = psum.tile([P, tokens.stop - tokens.start], F32, name="c_bank%d" % tokens.start)
            nc.tensor.matmul_mx(
                out=bank[:],
                lhsT=g_codes[:].bitcast(FP8X4),
                lhsT_scale=g_scales[:],
                rhs=v_codes[:, tokens].bitcast(FP8X4),
                rhs_scale=v_scales[:, tokens],
                start=True,
                stop=True,
            )
            return bank

        c_parts = (slice(0, 2 * CHUNK), slice(2 * CHUNK, 3 * CHUNK), slice(3 * CHUNK, 4 * CHUNK))
        quantize_values(0, round_values(0))
        v1_grouped = round_values(1)
        g_grouped, g_codes, g_scales = row_operand("g", g_raw)
        neg_m = keep.tile([P, 1], F32, name="neg_m")
        rp = keep.tile([P, SLOTS], F32, name="rp")
        rp_centred = keep.tile([P, SLOTS], F32, name="rp_centred")
        quantize_values(1, v1_grouped)
        quantize(g_grouped, g_codes[:], g_scales[:])
        c_banks = [score_values(c_parts[0])]
        v2_grouped = round_values(2)

        t_slots = keep.tile([P, SLOTS + 2 * LINE], F32, name="t_slots", tag="v_raw2", align_bytes=64)
        nc.gpsimd.memset(t_slots[:, SLOTS : SLOTS + 1], 0.0)
        neg_r = t_slots[:, SLOTS + LINE : SLOTS + LINE + 1]
        nc.vector.reciprocal(out=neg_r, in_=neg_z[:])
        nc.scalar.activation(out=rp[:], in_=p[:, 0:SLOTS], func=ACT.Copy, scale=neg_r)
        quantize_values(2, v2_grouped)
        c_banks.append(score_values(c_parts[1]))
        v3_grouped = round_values(3)
        nc.vector.tensor_copy(out=t_slots[:, 0:SLOTS], in_=ta_sb[:].indirect(offsets[:]))
        quantize_values(3, v3_grouped)
        c_banks.append(score_values(c_parts[2]))

        rpt = keep.tile([P, SLOTS + LINE], F32, name="rpt", tag="v3_grouped", align_bytes=64)
        nc.vector.scalar_tensor_tensor(
            out=rpt[:, 0:SLOTS], in0=t_slots[:, 0:SLOTS], scalar=neg_r, in1=p[:, 0:SLOTS], op0=ALU.mult, op1=ALU.mult, accum_out=neg_m[:]
        )
        nc.vector.scalar_tensor_tensor(out=rp_centred[:], in0=rp[:], scalar=neg_m[:], in1=rpt[:, 0:SLOTS], op0=ALU.mult, op1=ALU.add)

        c_sb = keep.tile([P, T], F32, name="c_sb", tag="v_raw3", align_bytes=64)
        for tokens, bank in zip(c_parts, c_banks):
            nc.scalar.copy(out=c_sb[:, tokens], in_=bank[:])
        nc.scalar.activation(out=pc[:, SLOTS : SLOTS + 1], in_=cp_col[:], func=ACT.Copy, scale=neg_r)

        term1 = keep.tile([P, SLOTS + LINE], F32, name="term1")
        terms12 = keep.tile([P, SLOTS], F32, name="terms12")
        term3 = keep.tile([P, SLOTS], F32, name="term3")
        term1_sum = keep.tile([P, 1], F32, name="term1_sum")
        pc_sum = keep.tile([P, 1], F32, name="pc_sum")
        nc.vector.tensor_tensor(out=pc[:, 0:SLOTS], in0=c_sb[:].indirect(offsets[:]), in1=rp[:], op=ALU.mult)
        nc.scalar.activation(out=summed[:, 0 : SLOTS + 1], in_=pc[:, 0 : SLOTS + 1], func=ACT.Copy, accum_out=pc_sum[:])
        nc.vector.scalar_tensor_tensor(
            out=term1[:, 0 : SLOTS + 1],
            in0=t_slots[:, 0 : SLOTS + 1],
            scalar=neg_m[:],
            in1=pc[:, 0 : SLOTS + 1],
            op0=ALU.add,
            op1=ALU.mult,
            accum_out=term1_sum[:],
        )
        nc.scalar.activation(out=term3[:], in_=rp_centred[:], func=ACT.Copy, scale=pc_sum[:])
        nc.vector.scalar_tensor_tensor(out=terms12[:], in0=rp[:], scalar=term1_sum[:], in1=term1[:, 0:SLOTS], op0=ALU.mult, op1=ALU.add)
        nc.vector.tensor_tensor(out=placed[:].indirect(offsets[:]), in0=terms12[:], in1=term3[:], op=ALU.add)

        first = 0
        for n, width in enumerate(OUT_PIECES):
            cols = slice(first, first + width)
            result = keep.tile([P, width], F32, name="result%d" % n)
            nc.vector.scalar_tensor_tensor(out=result[:], in0=placed[:, cols], scalar=-OUT_SCALE, in1=base_sb[:, cols], op0=ALU.mult, op1=ALU.add)
            queue = nc.sync if n % 2 == 0 else nc.scalar
            queue.dma_start(out=out[:, cols], in_=result[:])
            first = first + width
